import numpy as np, ml_dtypes
CORES = [10,34,74,98]
N = 4
import mx_ref
NC, G = 384, 4
M = NC // N
C = np.float32(0.041)
BF = ml_dtypes.bfloat16
def cut(t, i, w=512):
    return t[:, w * i:w * i + w]
def tile(rs):
    return np.stack(rs, axis=2).reshape(128, -1).astype(BF)
def layer(w, X):
    out = []
    for i in range(G):
        for t in range(len(X)):
            p = mx_ref.matmul(mx_ref.quantize(cut(w, len(X) * i + t)), X[t])
            z = p if t == 0 else z + p
        out.append(z)
    return out
def act(Z):
    return [np.maximum(z, 0) * C for z in Z]
def setup_inputs(rng):
    def f(*shape):
        return mx_ref.flush((rng.standard_normal(shape, dtype=np.float32) * np.exp2(rng.integers(-2, 3, shape[:-1] + (1,)))).astype(BF))
    return {"x": f(N, 128, 4 * NC), "w1": f(N, 128, G * 512), "w2": f(N, 128, 512)}
def setup_inputs_blocks(rng):
    d = setup_inputs(rng)
    for k in ("x", "w1", "w2"): d[k] = mx_ref.spread(d[k], rng, 4)
    return d
def setup_inputs_wide(rng):
    d = setup_inputs(rng)
    for k in ("x", "w1", "w2"): d[k] = mx_ref.flush((d[k].astype(np.float32) * np.exp2(rng.integers(-8, 9, (N, 1, 1))).astype(np.float32)).astype(BF))
    return d
def setup_inputs_zeros(rng):
    d = setup_inputs(rng); v = d["x"].reshape(N, 128, -1, 4).copy()
    v[np.broadcast_to((rng.random((N, 1, v.shape[2], 1)) < 0.33), v.shape)] = 0
    d["x"] = v.reshape(d["x"].shape)
    return d
def reference(x, w1, w2):
    h = [tile(act(layer(w1[j], [mx_ref.quantize(x[j])]))) for j in range(N)]
    y = np.zeros((N, 128, NC), np.float32)
    for r in range(N):
        t = np.concatenate([cut(h[j], r, 4 * M) for j in range(N)], axis=1)
        y[r] = mx_ref.matmul(mx_ref.quantize(w2[r]), mx_ref.quantize(t))
    return {"y": y}

@@ -1,0 +1,218 @@
+import numpy as np
+from concourse.bass import DstId, RemoteDMATransfer
+from concourse.mybir import dt, AluOpType, ActivationFunctionType
+
+N, NC, G = 4, 384, 4
+RUN = NC // N
+TW = 128
+PAD = TW - RUN
+BANK = 512
+C = float(np.float32(0.041))
+SW = TW + 2 * RUN
+LAND = {1: TW, 3: TW + RUN, 2: TW + 2 * RUN}
+
+SCRATCH = {
+    "xb": ("sbuf", [128, 4 * (SW + RUN)], "bfloat16"),
+    "w1b": ("sbuf", [128, G * 4 * TW], "bfloat16"),
+    "w2b": ("sbuf", [128, 4 * TW], "bfloat16"),
+    "xq": ("sbuf", [128, SW], "float8_e4m3fn_x4"), "xs": ("sbuf", [128, SW], "uint8"),
+    "xq2": ("sbuf", [128, TW], "float8_e4m3fn_x4"), "xs2": ("sbuf", [128, TW], "uint8"),
+    "w1q": ("sbuf", [128, G * TW], "float8_e4m3fn_x4"), "w1s": ("sbuf", [128, G * TW], "uint8"),
+    "w2q": ("sbuf", [128, TW], "float8_e4m3fn_x4"), "w2s": ("sbuf", [128, TW], "uint8"),
+    "hb": ("sbuf", [128, 4 * SW], "bfloat16"),
+    "hb2": ("sbuf", [128, 4 * TW], "bfloat16"),
+    "hq": ("sbuf", [128, SW], "float8_e4m3fn_x4"), "hs": ("sbuf", [128, SW], "uint8"),
+    "bq": ("sbuf", [128, PAD + NC], "float8_e4m3fn_x4"), "bs": ("sbuf", [128, PAD + NC], "uint8"),
+    "ysb": ("sbuf", [128, NC], "float32"),
+    "z": ("psum", [128, 8 * BANK], "float32"),
+}
+SEMAPHORES = (["lx0", "lx1", "lx2", "lw1a", "lw1b", "lw2", "qx0", "qx1", "qx2", "qv2", "qh0", "qh1", "qh2",
+               "act0", "act1", "act2", "arr_a", "arr_bc", "sent", "t0", "t1", "cp0", "cp1", "st0", "st1"]
+              + ["qw%d" % i for i in range(G)] + ["mm%d_%d" % (p, i) for p in range(3) for i in range(G)])
+
+
+def _plan(r):
+    a, b, c = [(r + k) % N for k in (1, 2, 3)]
+    if RUN * a + TW <= NC:
+        first = [(0, RUN * a, TW)]
+        pos = {a: 0, b: RUN, c: 2 * RUN}
+        rest = [(TW, RUN * a + TW, 2 * RUN - TW), (2 * RUN, RUN * c, RUN)]
+    else:
+        first = [(0, NC - TW, TW)]
+        pos = {a: PAD, b: TW, c: TW + RUN}
+        rest = [(TW, RUN * b, RUN), (TW + RUN, RUN * c, RUN)]
+    if rest[0][1] + rest[0][2] == rest[1][1]:
+        rest = [(rest[0][0], rest[0][1], rest[0][2] + rest[1][2])]
+    own = pos[c] + RUN
+    pos[r] = own
+    return first, rest, [(own, RUN * r, RUN)], pos
+
+
+def _bits(engines):
+    m = 0
+    for e in engines:
+        m |= 1 << e
+    return m
+
+
+def rank_program(g, core, T, topo):
+    r = T.rank_of(core)
+    if r is None:
+        return
+    S = T.sem
+    v, sc, te, sy = g.vector, g.scalar, g.tensor, g.sync
+    first, rest, last, pos = _plan(r)
+    own = pos[r]
+    a, b, c = [(r + k) % N for k in (1, 2, 3)]
+    u8 = dt.uint8
+
+    turn = [0]
+
+    def load(out, in_, sem):
+        q = (sy, sc)[turn[0] % 2]
+        turn[0] += 1
+        q.dma_start(out, in_).then_inc(sem, 16)
+
+    def load_x(group, sem):
+        for (s, h, w) in group:
+            load(T.xb[:, 4 * s:4 * (s + w)], T.x[:, 4 * h:4 * (h + w)], sem)
+        return 16 * len(group)
+
+    half = G * 4 * TW // 2
+    n0 = load_x(first, S.lx0)
+    load(T.w1b[:, 0:half], T.w1[:, 0:half], S.lw1a)
+    load(T.w1b[:, half:2 * half], T.w1[:, half:2 * half], S.lw1b)
+    n1 = load_x(rest, S.lx1)
+    n2 = load_x(last, S.lx2)
+    load(T.w2b[:], T.w2[:], S.lw2)
+
+    pieces = [
+        (T.xq[:, 0:TW], T.xs[:, 0:TW], TW, 0, T.hb, 0),
+        (T.xq[:, TW:own], T.xs[:, TW:own], own - TW, G, T.hb, TW),
+        (T.xq2[:], T.xs2[:], TW, 0, T.hb2, 0),
+    ]
+
+    def relu(eng, p, i):
+        _, _, w, bank, hb, s = pieces[p]
+        src = T.z[:, BANK * (bank + i):BANK * (bank + i) + w]
+        dst = hb[:, 4 * s + i:4 * (s + w):4]
+        eng.wait_ge(S["mm%d_%d" % (p, i)], 1)
+        if eng is sc:
+            ins = sc.activation(dst, src, ActivationFunctionType.Relu, scale=C)
+        else:
+            ins = v.tensor_scalar(dst, src, 0.0, C, AluOpType.max, AluOpType.mult)
+        ins.then_inc(S["act%d" % p], 1)
+
+    v.wait_ge(S.lx0, n0)
+    v.quantize_mx(T.xq[:, 0:TW], T.xs[:, 0:TW], T.xb[:, 0:4 * TW]).then_inc(S.qx0, 1)
+    for i in range(G):
+        if i == 0:
+            v.wait_ge(S.lw1a, 16)
+        if i == G // 2:
+            v.wait_ge(S.lw1b, 16)
+        v.quantize_mx(T.w1q[:, TW * i:TW * (i + 1)], T.w1s[:, TW * i:TW * (i + 1)],
+                      T.w1b[:, 4 * TW * i:4 * TW * (i + 1)]).then_inc(S["qw%d" % i], 1)
+    v.wait_ge(S.act0, G)
+    v.quantize_mx(T.hq[:, 0:TW], T.hs[:, 0:TW], T.hb[:, 0:4 * TW]).then_inc(S.qh0, 1)
+    v.wait_ge(S.lx1, n1)
+    v.quantize_mx(T.xq[:, TW:own], T.xs[:, TW:own], T.xb[:, 4 * TW:4 * own]).then_inc(S.qx1, 1)
+    relu(v, 1, 1)
+    relu(v, 1, 3)
+    v.wait_ge(S.act1, G)
+    v.quantize_mx(T.hq[:, TW:own], T.hs[:, TW:own], T.hb[:, 4 * TW:4 * own]).then_inc(S.qh1, 1)
+    v.wait_ge(S.lx2, n2)
+    v.quantize_mx(T.xq2[:], T.xs2[:], T.xb[:, 4 * (own - PAD):4 * (own + RUN)]).then_inc(S.qx2, 1)
+    v.wait_ge(S.lw2, 16)
+    v.quantize_mx(T.w2q[:], T.w2s[:], T.w2b[:]).then_inc(S.qv2, 1)
+    relu(v, 2, 1)
+    relu(v, 2, 3)
+    v.wait_ge(S.act2, G)
+    v.quantize_mx(T.bq[:, 0:TW], T.bs[:, 0:TW], T.hb2[:]).then_inc(S.qh2, 1)
+    v.wait_ge(S.t0, 1)
+    v.tensor_copy(T.ysb[:, RUN:2 * RUN], T.z[:, BANK * G:BANK * G + RUN]).then_inc(S.cp0, 1)
+    v.tensor_copy(T.ysb[:, 0:RUN], T.z[:, BANK * G + RUN:BANK * G + 2 * RUN]).then_inc(S.cp0, 1)
+    v.wait_ge(S.t1, 1)
+    v.tensor_copy(T.ysb[:, 2 * RUN:4 * RUN], T.z[:, BANK * (G + 1):BANK * (G + 1) + 2 * RUN]).then_inc(S.cp1, 1)
+
+    for i in range(G):
+        relu(sc, 0, i)
+    for p in (1, 2):
+        relu(sc, p, 0)
+        relu(sc, p, 2)
+
+    for p in range(3):
+        xq, xs, w, bank, _, _ = pieces[p]
+        te.wait_ge(S["qx%d" % p], 1)
+        if p == 2:
+            te.wait_ge(S.act0, G)
+        for i in range(G):
+            if p == 0:
+                te.wait_ge(S["qw%d" % i], 1)
+            te.matmul_mx(T.z[:, BANK * (bank + i):BANK * (bank + i) + w], T.w1q[:, TW * i:TW * (i + 1)],
+                         T.w1s[:, TW * i:TW * (i + 1)], xq, xs, True, True).then_inc(S["mm%d_%d" % (p, i)], 1)
+    te.wait_ge(S.act1, G)
+    te.wait_ge(S.qv2, 1)
+    te.wait_ge(S.qh2, 1)
+
+    def halves(dst):
+        m = topo.mask(core, dst)
+        es = [e for e in range(m.bit_length()) if (m >> e) & 1]
+        return es[0::2], es[1::2]
+
+    def where(k):
+        dst = T.cores[(r + k) % N]
+        assert topo.may_write(core, dst)
+        rid, pid, _ = topo.addr(dst)
+        return dst, rid, pid
+
+    def views(k):
+        s, d = pos[(r + k) % N], LAND[k]
+        return ((T.hq[:, s:s + RUN].bitcast(u8), T.bq[:, d:d + RUN].bitcast(u8)),
+                (T.hs[:, s:s + RUN], T.bs[:, d:d + RUN]))
+
+    sent = 0
+    got_a = 0
+    g.wait_ge(S.qh0, 1)
+    dst, rid, pid = where(1)
+    for (src_ap, dst_ap), es in zip(views(1), halves(dst)):
+        g.remote_dma(out_ap=dst_ap, in_ap=src_ap, remote_sem=S.arr_a, local_sem=S.sent, pid=pid, routing_id=rid,
+                     dma_engine_mask=_bits(es))
+        sent += len(es)
+        got_a += len(es)
+    g.wait_ge(S.qh1, 1)
+    got_bc = 0
+    for part in (0, 1):
+        trs = []
+        for n, k in enumerate((2, 3)):
+            dst, rid, pid = where(k)
+            es = halves(dst)[(n + part) % 2]
+            src_ap, dst_ap = views(k)[part]
+            trs.append(RemoteDMATransfer(dst_ids=[DstId(rid=rid, pnc=pid)], dma_engine_mask=_bits(es),
+                                         remote_sem=S.arr_bc, src=src_ap, dst=dst_ap))
+            sent += len(es)
+            got_bc += len(es)
+        g.remote_dma_fused(trs, local_sem=S.sent)
+    g.wait_ge(S.sent, sent)
+
+    te.wait_ge(S.arr_a, got_a)
+    te.matmul_mx(T.z[:, BANK * G:BANK * G + 2 * RUN], T.w2q[:], T.w2s[:], T.bq[:, PAD:PAD + 2 * RUN],
+                 T.bs[:, PAD:PAD + 2 * RUN], True, True).then_inc(S.t0, 1)
+    te.wait_ge(S.arr_bc, got_bc)
+    te.matmul_mx(T.z[:, BANK * (G + 1):BANK * (G + 1) + 2 * RUN], T.w2q[:], T.w2s[:],
+                 T.bq[:, PAD + 2 * RUN:PAD + 4 * RUN], T.bs[:, PAD + 2 * RUN:PAD + 4 * RUN], True, True).then_inc(S.t1, 1)
+
+    def store(base, u, cp, ncp, st):
+        w = (u + 1) % N
+        if w == u + 1:
+            jobs = [(sy, base, RUN * u, 2 * RUN)]
+        else:
+            jobs = [(sy, base, RUN * u, RUN), (sc, base + RUN, RUN * w, RUN)]
+        for q, s, d, n in jobs:
+            q.wait_ge(cp, ncp)
+            q.dma_start(T.y[:, d:d + n], T.ysb[:, s:s + n]).then_inc(st, 16)
+        return 16 * len(jobs)
+
+    m0 = store(0, (r + 3) % N, S.cp0, 2, S.st0)
+    m1 = store(2 * RUN, (r + 1) % N, S.cp1, 1, S.st1)
+    sy.wait_ge(S.st0, m0)
+    sy.wait_ge(S.st1, m1)

@@ -8,44 +8,47 @@ TW = 128
 PAD = TW - RUN
 BANK = 512
 C = float(np.float32(0.041))
-SW = TW + 2 * RUN
-LAND = {1: TW, 3: TW + RUN, 2: TW + 2 * RUN}
+END = 3 * TW
+ALL = END + (N - 1) * RUN
+assert 3 * PAD == RUN
 
 SCRATCH = {
-    "xb": ("sbuf", [128, 4 * (SW + RUN)], "bfloat16"),
+    "xb": ("sbuf", [128, 4 * END], "bfloat16"),
     "w1b": ("sbuf", [128, G * 4 * TW], "bfloat16"),
     "w2b": ("sbuf", [128, 4 * TW], "bfloat16"),
-    "xq": ("sbuf", [128, SW], "float8_e4m3fn_x4"), "xs": ("sbuf", [128, SW], "uint8"),
-    "xq2": ("sbuf", [128, TW], "float8_e4m3fn_x4"), "xs2": ("sbuf", [128, TW], "uint8"),
+    "xq": ("sbuf", [128, END], "float8_e4m3fn_x4"), "xs": ("sbuf", [128, END], "uint8"),
     "w1q": ("sbuf", [128, G * TW], "float8_e4m3fn_x4"), "w1s": ("sbuf", [128, G * TW], "uint8"),
     "w2q": ("sbuf", [128, TW], "float8_e4m3fn_x4"), "w2s": ("sbuf", [128, TW], "uint8"),
-    "hb": ("sbuf", [128, 4 * SW], "bfloat16"),
-    "hb2": ("sbuf", [128, 4 * TW], "bfloat16"),
-    "hq": ("sbuf", [128, SW], "float8_e4m3fn_x4"), "hs": ("sbuf", [128, SW], "uint8"),
-    "bq": ("sbuf", [128, PAD + NC], "float8_e4m3fn_x4"), "bs": ("sbuf", [128, PAD + NC], "uint8"),
+    "hb": ("sbuf", [128, 4 * END], "bfloat16"),
+    "hq": ("sbuf", [128, ALL], "float8_e4m3fn_x4"), "hs": ("sbuf", [128, ALL], "uint8"),
     "ysb": ("sbuf", [128, NC], "float32"),
     "z": ("psum", [128, 8 * BANK], "float32"),
 }
-SEMAPHORES = (["lx0", "lx1", "lx2", "lw1a", "lw1b", "lw2", "qx0", "qx1", "qx2", "qv2", "qh0", "qh1", "qh2",
-               "act0", "act1", "act2", "arr_a", "arr_bc", "sent", "t0", "t1", "cp0", "cp1", "st0", "st1"]
+SEMAPHORES = (["lx0", "lx1", "lx2", "lw1a", "lw1b", "lw1c", "lw2", "qx0", "qx1", "qx2", "qv2", "qh0", "qh1", "qh2",
+               "act0", "act1", "act2", "arr1", "arr2", "arr3", "sent", "to", "t12", "t3", "cpo", "cpa", "cpb", "cpc",
+               "sta", "stb", "stc"]
               + ["qw%d" % i for i in range(G)] + ["mm%d_%d" % (p, i) for p in range(3) for i in range(G)])
 
 
-def _plan(r):
-    a, b, c = [(r + k) % N for k in (1, 2, 3)]
-    if RUN * a + TW <= NC:
-        first = [(0, RUN * a, TW)]
-        pos = {a: 0, b: RUN, c: 2 * RUN}
-        rest = [(TW, RUN * a + TW, 2 * RUN - TW), (2 * RUN, RUN * c, RUN)]
-    else:
-        first = [(0, NC - TW, TW)]
-        pos = {a: PAD, b: TW, c: TW + RUN}
-        rest = [(TW, RUN * b, RUN), (TW + RUN, RUN * c, RUN)]
-    if rest[0][1] + rest[0][2] == rest[1][1]:
-        rest = [(rest[0][0], rest[0][1], rest[0][2] + rest[1][2])]
-    own = pos[c] + RUN
-    pos[r] = own
-    return first, rest, [(own, RUN * r, RUN)], pos
+def _order(r, cores, topo):
+    here = topo.chip(cores[r])
+    return sorted([r ^ 1, r ^ 3, r ^ 2], key=lambda d: 1 if topo.same_plane(here, topo.chip(cores[d])) else 0)
+
+
+def _plan(r, order):
+    out = []
+    for d in order:
+        if d == (r + N - 1) % N:
+            s, run, segs = 0, 0, [(0, RUN * d, RUN), (RUN, RUN * r, PAD)]
+        elif d == (r + 1) % N:
+            s, run, segs = TW, TW + PAD, [(TW, RUN * r + 2 * PAD, PAD), (TW + PAD, RUN * d, RUN)]
+        else:
+            s, run, segs = 2 * TW, 2 * TW, [(2 * TW, RUN * d, RUN), (2 * TW + RUN, RUN * r + PAD, PAD)]
+        if segs[0][1] + segs[0][2] == segs[1][1]:
+            segs = [(segs[0][0], segs[0][1], TW)]
+        out.append((s, run, segs))
+    assert out[2][0] == 2 * TW and len(out[0][2]) == 1
+    return out
 
 
 def _bits(engines):
@@ -61,9 +64,10 @@ def rank_program(g, core, T, topo):
         return
     S = T.sem
     v, sc, te, sy = g.vector, g.scalar, g.tensor, g.sync
-    first, rest, last, pos = _plan(r)
-    own = pos[r]
-    a, b, c = [(r + k) % N for k in (1, 2, 3)]
+    order = _order(r, T.cores, topo)
+    plan = _plan(r, order)
+    senders = [[s for s in range(N) if s != r and _order(s, T.cores, topo)[p] == r][0] for p in range(3)]
+    banks = (0, G, 0)
     u8 = dt.uint8
 
     turn = [0]
@@ -73,29 +77,24 @@ def rank_program(g, core, T, topo):
         turn[0] += 1
         q.dma_start(out, in_).then_inc(sem, 16)
 
-    def load_x(group, sem):
-        for (s, h, w) in group:
-            load(T.xb[:, 4 * s:4 * (s + w)], T.x[:, 4 * h:4 * (h + w)], sem)
-        return 16 * len(group)
+    def load_x(p):
+        for (s, h, w) in plan[p][2]:
+            load(T.xb[:, 4 * s:4 * (s + w)], T.x[:, 4 * h:4 * (h + w)], S["lx%d" % p])
+        return 16 * len(plan[p][2])
 
-    half = G * 4 * TW // 2
-    n0 = load_x(first, S.lx0)
-    load(T.w1b[:, 0:half], T.w1[:, 0:half], S.lw1a)
-    load(T.w1b[:, half:2 * half], T.w1[:, half:2 * half], S.lw1b)
-    n1 = load_x(rest, S.lx1)
-    n2 = load_x(last, S.lx2)
+    nx = [0, 0, 0]
+    nx[0] = load_x(0)
+    w1cuts = ((0, 2, S.lw1a), (2, 3, S.lw1b), (3, 4, S.lw1c))
+    for i0, i1, sem in w1cuts:
+        load(T.w1b[:, 4 * TW * i0:4 * TW * i1], T.w1[:, 4 * TW * i0:4 * TW * i1], sem)
+    nx[1] = load_x(1)
+    nx[2] = load_x(2)
     load(T.w2b[:], T.w2[:], S.lw2)
 
-    pieces = [
-        (T.xq[:, 0:TW], T.xs[:, 0:TW], TW, 0, T.hb, 0),
-        (T.xq[:, TW:own], T.xs[:, TW:own], own - TW, G, T.hb, TW),
-        (T.xq2[:], T.xs2[:], TW, 0, T.hb2, 0),
-    ]
-
     def relu(eng, p, i):
-        _, _, w, bank, hb, s = pieces[p]
-        src = T.z[:, BANK * (bank + i):BANK * (bank + i) + w]
-        dst = hb[:, 4 * s + i:4 * (s + w):4]
+        s = plan[p][0]
+        src = T.z[:, BANK * (banks[p] + i):BANK * (banks[p] + i) + TW]
+        dst = T.hb[:, 4 * s + i:4 * (s + TW):4]
         eng.wait_ge(S["mm%d_%d" % (p, i)], 1)
         if eng is sc:
             ins = sc.activation(dst, src, ActivationFunctionType.Relu, scale=C)
@@ -103,116 +102,121 @@ def rank_program(g, core, T, topo):
             ins = v.tensor_scalar(dst, src, 0.0, C, AluOpType.max, AluOpType.mult)
         ins.then_inc(S["act%d" % p], 1)
 
-    v.wait_ge(S.lx0, n0)
-    v.quantize_mx(T.xq[:, 0:TW], T.xs[:, 0:TW], T.xb[:, 0:4 * TW]).then_inc(S.qx0, 1)
-    for i in range(G):
-        if i == 0:
-            v.wait_ge(S.lw1a, 16)
-        if i == G // 2:
-            v.wait_ge(S.lw1b, 16)
-        v.quantize_mx(T.w1q[:, TW * i:TW * (i + 1)], T.w1s[:, TW * i:TW * (i + 1)],
-                      T.w1b[:, 4 * TW * i:4 * TW * (i + 1)]).then_inc(S["qw%d" % i], 1)
-    v.wait_ge(S.act0, G)
-    v.quantize_mx(T.hq[:, 0:TW], T.hs[:, 0:TW], T.hb[:, 0:4 * TW]).then_inc(S.qh0, 1)
-    v.wait_ge(S.lx1, n1)
-    v.quantize_mx(T.xq[:, TW:own], T.xs[:, TW:own], T.xb[:, 4 * TW:4 * own]).then_inc(S.qx1, 1)
-    relu(v, 1, 1)
+    def quant_x(p):
+        s = plan[p][0]
+        v.wait_ge(S["lx%d" % p], nx[p])
+        v.quantize_mx(T.xq[:, s:s + TW], T.xs[:, s:s + TW], T.xb[:, 4 * s:4 * (s + TW)]).then_inc(S["qx%d" % p], 1)
+
+    def quant_h(p):
+        s = plan[p][0]
+        v.wait_ge(S["act%d" % p], G)
+        v.quantize_mx(T.hq[:, s:s + TW], T.hs[:, s:s + TW], T.hb[:, 4 * s:4 * (s + TW)]).then_inc(S["qh%d" % p], 1)
+
+    BO, B12, B3 = BANK * G, BANK * (G + 1), BANK * (G + 2)
+    own = RUN * r
+
+    quant_x(0)
+    for i0, i1, sem in w1cuts:
+        v.wait_ge(sem, 16)
+        for i in range(i0, i1):
+            v.quantize_mx(T.w1q[:, TW * i:TW * (i + 1)], T.w1s[:, TW * i:TW * (i + 1)],
+                          T.w1b[:, 4 * TW * i:4 * TW * (i + 1)]).then_inc(S["qw%d" % i], 1)
+    quant_h(0)
+    quant_x(1)
+    quant_x(2)
     relu(v, 1, 3)
-    v.wait_ge(S.act1, G)
-    v.quantize_mx(T.hq[:, TW:own], T.hs[:, TW:own], T.hb[:, 4 * TW:4 * own]).then_inc(S.qh1, 1)
-    v.wait_ge(S.lx2, n2)
-    v.quantize_mx(T.xq2[:], T.xs2[:], T.xb[:, 4 * (own - PAD):4 * (own + RUN)]).then_inc(S.qx2, 1)
-    v.wait_ge(S.lw2, 16)
-    v.quantize_mx(T.w2q[:], T.w2s[:], T.w2b[:]).then_inc(S.qv2, 1)
+    quant_h(1)
     relu(v, 2, 1)
     relu(v, 2, 3)
-    v.wait_ge(S.act2, G)
-    v.quantize_mx(T.bq[:, 0:TW], T.bs[:, 0:TW], T.hb2[:]).then_inc(S.qh2, 1)
-    v.wait_ge(S.t0, 1)
-    v.tensor_copy(T.ysb[:, RUN:2 * RUN], T.z[:, BANK * G:BANK * G + RUN]).then_inc(S.cp0, 1)
-    v.tensor_copy(T.ysb[:, 0:RUN], T.z[:, BANK * G + RUN:BANK * G + 2 * RUN]).then_inc(S.cp0, 1)
-    v.wait_ge(S.t1, 1)
-    v.tensor_copy(T.ysb[:, 2 * RUN:4 * RUN], T.z[:, BANK * (G + 1):BANK * (G + 1) + 2 * RUN]).then_inc(S.cp1, 1)
+    quant_h(2)
+    v.wait_ge(S.lw2, 16)
+    v.quantize_mx(T.w2q[:], T.w2s[:], T.w2b[:]).then_inc(S.qv2, 1)
+    v.wait_ge(S.t12, 1)
+    y0, y1, y2 = [RUN * s for s in senders]
+    v.tensor_copy(T.ysb[:, own + PAD:own + 2 * PAD], T.z[:, B12:B12 + PAD]).then_inc(S.cpa, 1)
+    v.tensor_copy(T.ysb[:, y0:y0 + RUN], T.z[:, B12 + PAD:B12 + PAD + RUN]).then_inc(S.cpa, 1)
+    v.tensor_copy(T.ysb[:, y1:y1 + RUN], T.z[:, B12 + PAD + RUN:B12 + PAD + 2 * RUN]).then_inc(S.cpb, 1)
+    v.wait_ge(S.t3, 1)
+    v.tensor_copy(T.ysb[:, y2:y2 + RUN], T.z[:, B3 + PAD:B3 + TW]).then_inc(S.cpc, 1)
 
     for i in range(G):
         relu(sc, 0, i)
-    for p in (1, 2):
-        relu(sc, p, 0)
-        relu(sc, p, 2)
+    for i in range(G - 1):
+        relu(sc, 1, i)
+    relu(sc, 2, 0)
+    relu(sc, 2, 2)
+    sc.wait_ge(S.to, 1)
+    sc.activation(T.ysb[:, own:own + PAD], T.z[:, BO + PAD:BO + 2 * PAD],
+                  ActivationFunctionType.Copy).then_inc(S.cpo, 1)
+    sc.activation(T.ysb[:, own + 2 * PAD:own + RUN], T.z[:, BO + 2 * PAD:BO + 3 * PAD],
+                  ActivationFunctionType.Copy).then_inc(S.cpo, 1)
 
     for p in range(3):
-        xq, xs, w, bank, _, _ = pieces[p]
+        s = plan[p][0]
         te.wait_ge(S["qx%d" % p], 1)
         if p == 2:
             te.wait_ge(S.act0, G)
         for i in range(G):
             if p == 0:
                 te.wait_ge(S["qw%d" % i], 1)
-            te.matmul_mx(T.z[:, BANK * (bank + i):BANK * (bank + i) + w], T.w1q[:, TW * i:TW * (i + 1)],
-                         T.w1s[:, TW * i:TW * (i + 1)], xq, xs, True, True).then_inc(S["mm%d_%d" % (p, i)], 1)
-    te.wait_ge(S.act1, G)
-    te.wait_ge(S.qv2, 1)
-    te.wait_ge(S.qh2, 1)
+            te.matmul_mx(T.z[:, BANK * (banks[p] + i):BANK * (banks[p] + i) + TW], T.w1q[:, TW * i:TW * (i + 1)],
+                         T.w1s[:, TW * i:TW * (i + 1)], T.xq[:, s:s + TW], T.xs[:, s:s + TW],
+                         True, True).then_inc(S["mm%d_%d" % (p, i)], 1)
 
-    def halves(dst):
-        m = topo.mask(core, dst)
+    def masks(src, dst, p):
+        m = topo.mask(src, dst)
         es = [e for e in range(m.bit_length()) if (m >> e) & 1]
-        return es[0::2], es[1::2]
-
-    def where(k):
-        dst = T.cores[(r + k) % N]
-        assert topo.may_write(core, dst)
-        rid, pid, _ = topo.addr(dst)
-        return dst, rid, pid
-
-    def views(k):
-        s, d = pos[(r + k) % N], LAND[k]
-        return ((T.hq[:, s:s + RUN].bitcast(u8), T.bq[:, d:d + RUN].bitcast(u8)),
-                (T.hs[:, s:s + RUN], T.bs[:, d:d + RUN]))
+        if p == 0:
+            return es[0::2], es[1::2]
+        return es, es
 
     sent = 0
-    got_a = 0
-    g.wait_ge(S.qh0, 1)
-    dst, rid, pid = where(1)
-    for (src_ap, dst_ap), es in zip(views(1), halves(dst)):
-        g.remote_dma(out_ap=dst_ap, in_ap=src_ap, remote_sem=S.arr_a, local_sem=S.sent, pid=pid, routing_id=rid,
-                     dma_engine_mask=_bits(es))
-        sent += len(es)
-        got_a += len(es)
-    g.wait_ge(S.qh1, 1)
-    got_bc = 0
-    for part in (0, 1):
-        trs = []
-        for n, k in enumerate((2, 3)):
-            dst, rid, pid = where(k)
-            es = halves(dst)[(n + part) % 2]
-            src_ap, dst_ap = views(k)[part]
-            trs.append(RemoteDMATransfer(dst_ids=[DstId(rid=rid, pnc=pid)], dma_engine_mask=_bits(es),
-                                         remote_sem=S.arr_bc, src=src_ap, dst=dst_ap))
+    for p in range(3):
+        dst = T.cores[order[p]]
+        assert topo.may_write(core, dst)
+        rid, pid, _ = topo.addr(dst)
+        s, d = plan[p][1], END + RUN * p
+        views = ((T.hq[:, s:s + RUN].bitcast(u8), T.hq[:, d:d + RUN].bitcast(u8)),
+                 (T.hs[:, s:s + RUN], T.hs[:, d:d + RUN]))
+        g.wait_ge(S["qh%d" % p], 1)
+        for (src_ap, dst_ap), es in zip(views, masks(core, dst, p)):
+            g.remote_dma(out_ap=dst_ap, in_ap=src_ap, remote_sem=S["arr%d" % (p + 1)], local_sem=S.sent, pid=pid,
+                         routing_id=rid, dma_engine_mask=_bits(es))
             sent += len(es)
-            got_bc += len(es)
-        g.remote_dma_fused(trs, local_sem=S.sent)
     g.wait_ge(S.sent, sent)
 
-    te.wait_ge(S.arr_a, got_a)
-    te.matmul_mx(T.z[:, BANK * G:BANK * G + 2 * RUN], T.w2q[:], T.w2s[:], T.bq[:, PAD:PAD + 2 * RUN],
-                 T.bs[:, PAD:PAD + 2 * RUN], True, True).then_inc(S.t0, 1)
-    te.wait_ge(S.arr_bc, got_bc)
-    te.matmul_mx(T.z[:, BANK * (G + 1):BANK * (G + 1) + 2 * RUN], T.w2q[:], T.w2s[:],
-                 T.bq[:, PAD + 2 * RUN:PAD + 4 * RUN], T.bs[:, PAD + 2 * RUN:PAD + 4 * RUN], True, True).then_inc(S.t1, 1)
+    def got(p):
+        return sum(len(es) for es in masks(T.cores[senders[p]], core, p))
 
-    def store(base, u, cp, ncp, st):
-        w = (u + 1) % N
-        if w == u + 1:
-            jobs = [(sy, base, RUN * u, 2 * RUN)]
-        else:
-            jobs = [(sy, base, RUN * u, RUN), (sc, base + RUN, RUN * w, RUN)]
-        for q, s, d, n in jobs:
-            q.wait_ge(cp, ncp)
-            q.dma_start(T.y[:, d:d + n], T.ysb[:, s:s + n]).then_inc(st, 16)
-        return 16 * len(jobs)
+    def layer2(bank, lo, hi, sem):
+        te.matmul_mx(T.z[:, bank:bank + hi - lo], T.w2q[:], T.w2s[:], T.hq[:, lo:hi], T.hs[:, lo:hi],
+                     True, True).then_inc(sem, 1)
 
-    m0 = store(0, (r + 3) % N, S.cp0, 2, S.st0)
-    m1 = store(2 * RUN, (r + 1) % N, S.cp1, 1, S.st1)
-    sy.wait_ge(S.st0, m0)
-    sy.wait_ge(S.st1, m1)
+    te.wait_ge(S.act1, G)
+    te.wait_ge(S.qh0, 1)
+    te.wait_ge(S.qh1, 1)
+    te.wait_ge(S.qv2, 1)
+    layer2(BO, TW - 2 * PAD, 2 * TW - 2 * PAD, S.to)
+    te.wait_ge(S.qh2, 1)
+    te.wait_ge(S.arr1, got(0))
+    te.wait_ge(S.arr2, got(1))
+    layer2(B12, END - PAD, END + 2 * RUN, S.t12)
+    te.wait_ge(S.arr3, got(2))
+    layer2(B3, ALL - TW, ALL, S.t3)
+
+    lo = min(own, y0)
+    if max(own, y0) == lo + RUN:
+        jobs = [(lo, 2 * RUN)]
+    else:
+        jobs = [(own, RUN), (y0, RUN)]
+    sy.wait_ge(S.cpo, 2)
+    sy.wait_ge(S.cpa, 2)
+    for c0, n in jobs:
+        sy.dma_start(T.y[:, c0:c0 + n], T.ysb[:, c0:c0 + n]).then_inc(S.sta, 16)
+    sy.wait_ge(S.cpb, 1)
+    sy.dma_start(T.y[:, y1:y1 + RUN], T.ysb[:, y1:y1 + RUN]).then_inc(S.stb, 16)
+    sy.wait_ge(S.cpc, 1)
+    sy.dma_start(T.y[:, y2:y2 + RUN], T.ysb[:, y2:y2 + RUN]).then_inc(S.stc, 16)
+    sy.wait_ge(S.sta, 16 * len(jobs))
+    sy.wait_ge(S.stb, 16)
+    sy.wait_ge(S.stc, 16)

import numpy as np
from concourse.bass import DstId, RemoteDMATransfer
from concourse.mybir import dt, AluOpType, ActivationFunctionType

N, NC, G = 4, 384, 4
RUN = NC // N
TW = 128
PAD = TW - RUN
BANK = 512
C = float(np.float32(0.041))
END = 3 * TW
ALL = END + (N - 1) * RUN
assert 3 * PAD == RUN

SCRATCH = {
    "xb": ("sbuf", [128, 4 * END], "bfloat16"),
    "w1b": ("sbuf", [128, G * 4 * TW], "bfloat16"),
    "w2b": ("sbuf", [128, 4 * TW], "bfloat16"),
    "xq": ("sbuf", [128, END], "float8_e4m3fn_x4"), "xs": ("sbuf", [128, END], "uint8"),
    "w1q": ("sbuf", [128, G * TW], "float8_e4m3fn_x4"), "w1s": ("sbuf", [128, G * TW], "uint8"),
    "w2q": ("sbuf", [128, TW], "float8_e4m3fn_x4"), "w2s": ("sbuf", [128, TW], "uint8"),
    "hb": ("sbuf", [128, 4 * END], "bfloat16"),
    "hq": ("sbuf", [128, ALL], "float8_e4m3fn_x4"), "hs": ("sbuf", [128, ALL], "uint8"),
    "ysb": ("sbuf", [128, NC], "float32"),
    "z": ("psum", [128, 8 * BANK], "float32"),
}
SEMAPHORES = (["lx0", "lx1", "lx2", "lw1a", "lw1b", "lw1c", "lw2", "qx0", "qx1", "qx2", "qv2", "qh0", "qh1", "qh2",
               "act0", "act1", "act2", "arr1", "arr2", "arr3", "sent", "to", "t12", "t3", "cpo", "cpa", "cpb", "cpc",
               "sta", "stb", "stc"]
              + ["qw%d" % i for i in range(G)] + ["mm%d_%d" % (p, i) for p in range(3) for i in range(G)])


def _order(r, cores, topo):
    here = topo.chip(cores[r])
    return sorted([r ^ 1, r ^ 3, r ^ 2], key=lambda d: 1 if topo.same_plane(here, topo.chip(cores[d])) else 0)


def _plan(r, order):
    out = []
    for d in order:
        if d == (r + N - 1) % N:
            s, run, segs = 0, 0, [(0, RUN * d, RUN), (RUN, RUN * r, PAD)]
        elif d == (r + 1) % N:
            s, run, segs = TW, TW + PAD, [(TW, RUN * r + 2 * PAD, PAD), (TW + PAD, RUN * d, RUN)]
        else:
            s, run, segs = 2 * TW, 2 * TW, [(2 * TW, RUN * d, RUN), (2 * TW + RUN, RUN * r + PAD, PAD)]
        if segs[0][1] + segs[0][2] == segs[1][1]:
            segs = [(segs[0][0], segs[0][1], TW)]
        out.append((s, run, segs))
    assert out[2][0] == 2 * TW and len(out[0][2]) == 1
    return out


def _bits(engines):
    m = 0
    for e in engines:
        m |= 1 << e
    return m


def rank_program(g, core, T, topo):
    r = T.rank_of(core)
    if r is None:
        return
    S = T.sem
    v, sc, te, sy = g.vector, g.scalar, g.tensor, g.sync
    order = _order(r, T.cores, topo)
    plan = _plan(r, order)
    senders = [[s for s in range(N) if s != r and _order(s, T.cores, topo)[p] == r][0] for p in range(3)]
    banks = (0, G, 0)
    u8 = dt.uint8

    turn = [0]

    def load(out, in_, sem):
        q = (sy, sc)[turn[0] % 2]
        turn[0] += 1
        q.dma_start(out, in_).then_inc(sem, 16)

    def load_x(p):
        for (s, h, w) in plan[p][2]:
            load(T.xb[:, 4 * s:4 * (s + w)], T.x[:, 4 * h:4 * (h + w)], S["lx%d" % p])
        return 16 * len(plan[p][2])

    nx = [0, 0, 0]
    nx[0] = load_x(0)
    w1cuts = ((0, 2, S.lw1a), (2, 3, S.lw1b), (3, 4, S.lw1c))
    for i0, i1, sem in w1cuts:
        load(T.w1b[:, 4 * TW * i0:4 * TW * i1], T.w1[:, 4 * TW * i0:4 * TW * i1], sem)
    nx[1] = load_x(1)
    nx[2] = load_x(2)
    load(T.w2b[:], T.w2[:], S.lw2)

    def relu(eng, p, i):
        s = plan[p][0]
        src = T.z[:, BANK * (banks[p] + i):BANK * (banks[p] + i) + TW]
        dst = T.hb[:, 4 * s + i:4 * (s + TW):4]
        eng.wait_ge(S["mm%d_%d" % (p, i)], 1)
        if eng is sc:
            ins = sc.activation(dst, src, ActivationFunctionType.Relu, scale=C)
        else:
            ins = v.tensor_scalar(dst, src, 0.0, C, AluOpType.max, AluOpType.mult)
        ins.then_inc(S["act%d" % p], 1)

    def quant_x(p):
        s = plan[p][0]
        v.wait_ge(S["lx%d" % p], nx[p])
        v.quantize_mx(T.xq[:, s:s + TW], T.xs[:, s:s + TW], T.xb[:, 4 * s:4 * (s + TW)]).then_inc(S["qx%d" % p], 1)

    def quant_h(p):
        s = plan[p][0]
        v.wait_ge(S["act%d" % p], G)
        v.quantize_mx(T.hq[:, s:s + TW], T.hs[:, s:s + TW], T.hb[:, 4 * s:4 * (s + TW)]).then_inc(S["qh%d" % p], 1)

    BO, B12, B3 = BANK * G, BANK * (G + 1), BANK * (G + 2)
    own = RUN * r

    quant_x(0)
    for i0, i1, sem in w1cuts:
        v.wait_ge(sem, 16)
        for i in range(i0, i1):
            v.quantize_mx(T.w1q[:, TW * i:TW * (i + 1)], T.w1s[:, TW * i:TW * (i + 1)],
                          T.w1b[:, 4 * TW * i:4 * TW * (i + 1)]).then_inc(S["qw%d" % i], 1)
    quant_h(0)
    quant_x(1)
    quant_x(2)
    relu(v, 1, 3)
    quant_h(1)
    relu(v, 2, 1)
    relu(v, 2, 3)
    quant_h(2)
    v.wait_ge(S.lw2, 16)
    v.quantize_mx(T.w2q[:], T.w2s[:], T.w2b[:]).then_inc(S.qv2, 1)
    v.wait_ge(S.t12, 1)
    y0, y1, y2 = [RUN * s for s in senders]
    v.tensor_copy(T.ysb[:, own + PAD:own + 2 * PAD], T.z[:, B12:B12 + PAD]).then_inc(S.cpa, 1)
    v.tensor_copy(T.ysb[:, y0:y0 + RUN], T.z[:, B12 + PAD:B12 + PAD + RUN]).then_inc(S.cpa, 1)
    v.tensor_copy(T.ysb[:, y1:y1 + RUN], T.z[:, B12 + PAD + RUN:B12 + PAD + 2 * RUN]).then_inc(S.cpb, 1)
    v.wait_ge(S.t3, 1)
    v.tensor_copy(T.ysb[:, y2:y2 + RUN], T.z[:, B3 + PAD:B3 + TW]).then_inc(S.cpc, 1)

    for i in range(G):
        relu(sc, 0, i)
    for i in range(G - 1):
        relu(sc, 1, i)
    relu(sc, 2, 0)
    relu(sc, 2, 2)
    sc.wait_ge(S.to, 1)
    sc.activation(T.ysb[:, own:own + PAD], T.z[:, BO + PAD:BO + 2 * PAD],
                  ActivationFunctionType.Copy).then_inc(S.cpo, 1)
    sc.activation(T.ysb[:, own + 2 * PAD:own + RUN], T.z[:, BO + 2 * PAD:BO + 3 * PAD],
                  ActivationFunctionType.Copy).then_inc(S.cpo, 1)

    for p in range(3):
        s = plan[p][0]
        te.wait_ge(S["qx%d" % p], 1)
        if p == 2:
            te.wait_ge(S.act0, G)
        for i in range(G):
            if p == 0:
                te.wait_ge(S["qw%d" % i], 1)
            te.matmul_mx(T.z[:, BANK * (banks[p] + i):BANK * (banks[p] + i) + TW], T.w1q[:, TW * i:TW * (i + 1)],
                         T.w1s[:, TW * i:TW * (i + 1)], T.xq[:, s:s + TW], T.xs[:, s:s + TW],
                         True, True).then_inc(S["mm%d_%d" % (p, i)], 1)

    def masks(src, dst, p):
        m = topo.mask(src, dst)
        es = [e for e in range(m.bit_length()) if (m >> e) & 1]
        if p == 0:
            return es[0::2], es[1::2]
        return es, es

    sent = 0
    for p in range(3):
        dst = T.cores[order[p]]
        assert topo.may_write(core, dst)
        rid, pid, _ = topo.addr(dst)
        s, d = plan[p][1], END + RUN * p
        views = ((T.hq[:, s:s + RUN].bitcast(u8), T.hq[:, d:d + RUN].bitcast(u8)),
                 (T.hs[:, s:s + RUN], T.hs[:, d:d + RUN]))
        g.wait_ge(S["qh%d" % p], 1)
        for (src_ap, dst_ap), es in zip(views, masks(core, dst, p)):
            g.remote_dma(out_ap=dst_ap, in_ap=src_ap, remote_sem=S["arr%d" % (p + 1)], local_sem=S.sent, pid=pid,
                         routing_id=rid, dma_engine_mask=_bits(es))
            sent += len(es)
    g.wait_ge(S.sent, sent)

    def got(p):
        return sum(len(es) for es in masks(T.cores[senders[p]], core, p))

    def layer2(bank, lo, hi, sem):
        te.matmul_mx(T.z[:, bank:bank + hi - lo], T.w2q[:], T.w2s[:], T.hq[:, lo:hi], T.hs[:, lo:hi],
                     True, True).then_inc(sem, 1)

    te.wait_ge(S.act1, G)
    te.wait_ge(S.qh0, 1)
    te.wait_ge(S.qh1, 1)
    te.wait_ge(S.qv2, 1)
    layer2(BO, TW - 2 * PAD, 2 * TW - 2 * PAD, S.to)
    te.wait_ge(S.qh2, 1)
    te.wait_ge(S.arr1, got(0))
    te.wait_ge(S.arr2, got(1))
    layer2(B12, END - PAD, END + 2 * RUN, S.t12)
    te.wait_ge(S.arr3, got(2))
    layer2(B3, ALL - TW, ALL, S.t3)

    lo = min(own, y0)
    if max(own, y0) == lo + RUN:
        jobs = [(lo, 2 * RUN)]
    else:
        jobs = [(own, RUN), (y0, RUN)]
    sy.wait_ge(S.cpo, 2)
    sy.wait_ge(S.cpa, 2)
    for c0, n in jobs:
        sy.dma_start(T.y[:, c0:c0 + n], T.ysb[:, c0:c0 + n]).then_inc(S.sta, 16)
    sy.wait_ge(S.cpb, 1)
    sy.dma_start(T.y[:, y1:y1 + RUN], T.ysb[:, y1:y1 + RUN]).then_inc(S.stb, 16)
    sy.wait_ge(S.cpc, 1)
    sy.dma_start(T.y[:, y2:y2 + RUN], T.ysb[:, y2:y2 + RUN]).then_inc(S.stc, 16)
    sy.wait_ge(S.sta, 16 * len(jobs))
    sy.wait_ge(S.stb, 16)
    sy.wait_ge(S.stc, 16)
